import numpy as np
import ml_dtypes


def mxq(x, axis, fmt="e4m3"):
    dtype, down = {"e4m3": (ml_dtypes.float8_e4m3fn, 7), "e5m2": (ml_dtypes.float8_e5m2, 14)}[fmt]
    v = np.moveaxis(np.asarray(x, np.float32).astype(ml_dtypes.bfloat16).astype(np.float64), axis, -1)
    blocks = v.reshape(v.shape[:-1] + (-1, 32))
    amax = np.abs(blocks).max(-1, keepdims=True)
    byte = np.maximum(np.where(amax > 0, np.frexp(amax)[1] - 1 + 127, 0) - down, 1)
    scale = np.exp2(byte - 127.0)
    codes = (blocks / scale).astype(np.float32).astype(dtype).astype(np.float64)
    return np.moveaxis((codes * scale).reshape(v.shape), -1, axis)


WIDE = False


def mx_kscale(k):
    if not WIDE:
        return np.ones(k)
    levels = np.array([10, -10, 5, -5, 0])
    if k % 512:
        return np.exp2(np.random.permutation(np.resize(levels, k // 32))).repeat(32)
    a = np.empty((k // 512, 16))
    for p in range(k // 512):
        a[p, :8] = np.random.permutation(np.resize(levels, 8))
        for g in range(8):
            far = levels[np.abs(levels - a[p, g]) >= 10]
            a[p, g + 8] = far[np.random.randint(len(far))]
    return np.exp2(a.ravel()).repeat(32)


def f64(x):
    return np.asarray(x).astype(np.float64)


def striped(idx):
    return np.tile(np.asarray(idx).reshape(-1, 16).T, (8, 1)).astype(np.uint16)


def unstriped(offs):
    return offs[:16].T.reshape(-1).astype(np.int64)


D, T, I, M = 512, 1024, 512, 512


def setup_inputs():
    n = np.random.standard_normal
    idx = np.random.permutation(T)[:I]
    fd = mx_kscale(D)
    return {
        "xs": (n((D, T))).astype(np.float32),
        "fa": (np.random.uniform(0.5, 1.5, (D, 1)) * fd[:, None]).astype(np.float32),
        "fb": (np.random.uniform(0.5, 1.5, (D, 1)) * fd[:, None]).astype(np.float32),
        "niv": ((-np.random.uniform(0.0, 0.5, (D, M)) / np.sqrt(D)) / fd[:, None]).astype(np.float32),
        "miv": (n((D, M)) * 0.3 / np.sqrt(D) / fd[:, None]).astype(np.float32),
        "con": (np.random.uniform(-1.0, 1.0, (1, M))).astype(np.float32),
        "offs": striped(idx),
    }


def reference(xs, fa, fb, niv, miv, con, offs):
    idx = unstriped(offs)
    x2 = np.square(f64(xs)[:, idx]) * f64(fa)
    x1 = f64(xs)[:, idx] * f64(fb)
    x2q = mxq(x2, 0, "e4m3")
    nivq = mxq(f64(niv), 0, "e4m3")
    x1q = mxq(x1, 0, "e4m3")
    mivq = mxq(f64(miv), 0, "e4m3")
    a = x2q.T @ nivq + x1q.T @ mivq
    s = a + f64(con)
    p = np.exp(s - np.max(s, axis=1, keepdims=True))
    y = p / np.sum(p, axis=1, keepdims=True) * 512.0
    return y

@@ -1,0 +1,145 @@
+from contextlib import ExitStack
+
+import concourse.mybir as mybir
+from concourse.masks import make_identity
+
+D, T, I, M = 512, 1024, 512, 512
+FLOPS = 2 * 2 * D * I * M
+
+F32 = mybir.dt.float32
+BF16 = mybir.dt.bfloat16
+U32 = mybir.dt.uint32
+U16 = mybir.dt.uint16
+U8 = mybir.dt.uint8
+FP8X4 = mybir.dt.float8_e4m3fn_x4
+ALU = mybir.AluOpType
+ACT = mybir.ActivationFunctionType
+AXIS = mybir.AxisListType
+
+P = 128
+PACK = 4
+HALF = 256
+RUN = 4
+
+
+def planes_view(ap):
+    return ap.rearrange("p t (c i) -> p c t i", i=RUN)
+
+
+def words_view(ap):
+    return ap.rearrange("p (c i) t -> p c t i", i=RUN)
+
+
+def tile_attend_mixtureresp_kernel(tc, xs, fa, fb, niv, miv, con, offs, out):
+    nc = tc.nc
+    with ExitStack() as ctx:
+        keep = ctx.enter_context(tc.tile_pool(name="keep", bufs=1))
+        psum = ctx.enter_context(tc.psum_pool(name="psum", bufs=1))
+
+        offsets = keep.tile([P, I // 16], U16, name="offsets")
+        nc.sync.dma_start(offsets[:], offs)
+        xs_planes = xs.rearrange("(p t) s -> p t s", t=PACK)
+        windows = [keep.tile([P, T], F32, name="window%d" % t) for t in range(PACK)]
+        for t in range(PACK):
+            nc.sync.dma_start(windows[t][:], xs_planes[:, t, :])
+        fa_t = keep.tile([P, PACK], F32, name="fa_t")
+        fb_t = keep.tile([P, PACK], F32, name="fb_t")
+        con_t = keep.tile([P, PACK], F32, name="con_t")
+        nc.scalar.dma_start(fb_t[:], fb.rearrange("(p t) o -> p (t o)", t=PACK))
+        nc.scalar.dma_start(fa_t[:], fa.rearrange("(p t) o -> p (t o)", t=PACK))
+        nc.scalar.dma_start(con_t[:], con.rearrange("o (p t) -> p (o t)", t=PACK))
+        raw = {}
+        for name, table in (("niv", niv), ("miv", miv)):
+            for h in range(2):
+                raw[name, h] = keep.tile([P, PACK, HALF], F32, name="raw_%s%d" % (name, h))
+                nc.sync.dma_start(
+                    raw[name, h][:],
+                    table.rearrange("(p t) m -> p t m", t=PACK)[:, :, h * HALF : (h + 1) * HALF],
+                )
+
+        ident = keep.tile([P, P], F32, name="ident")
+        make_identity(nc, ident[:])
+        con_bank = psum.tile([P, PACK, P], F32, name="con_bank")
+        for t in range(PACK):
+            nc.tensor.transpose(con_bank[:, t, :], con_t[:, t : t + 1].to_broadcast([P, P]), ident[:])
+        con_rows = keep.tile([P, P, PACK], F32, name="con_rows")
+        nc.scalar.activation(con_rows[:], con_bank[:].rearrange("p t n -> p n t"), ACT.Copy)
+
+        picked = keep.tile([P, PACK, I], F32, name="picked")
+        squares = keep.tile([P, PACK, I], F32, name="squares")
+        x1_planes = keep.tile([P, PACK, HALF], BF16, name="x1_planes")
+        for t in range(PACK):
+            nc.vector.tensor_copy(picked[:, t, :], windows[t][:].indirect(offsets[:]))
+            nc.scalar.activation(squares[:, t, :], picked[:, t, :], ACT.Square)
+            nc.scalar.activation(x1_planes[:, t, :], picked[:, t, HALF:], ACT.Copy, scale=fb_t[:, t : t + 1])
+
+        def per_feature(col):
+            return col[:].rearrange("p (a t b) -> p a t b", a=1, b=1).to_broadcast([P, HALF // RUN, PACK, RUN])
+
+        def quantize(name, grouped):
+            width = grouped.shape[1]
+            codes = keep.tile([P, width], U32, name="codes_" + name, align_bytes=64)
+            scales = keep.tile([P, width], U8, name="scales_" + name, align_bytes=64)
+            nc.vector.quantize_mx(
+                out=codes[:].bitcast(FP8X4), scales=scales[:], in_=grouped[:].rearrange("p w t -> p (w t)")
+            )
+            return codes, scales
+
+        grouped = {}
+        for name in ("x1", "x2", "niv", "miv"):
+            for h in range(2):
+                grouped[name, h] = keep.tile([P, HALF, PACK], BF16, name="grouped_%s%d" % (name, h), align_bytes=64)
+        quant = {}
+
+        nc.vector.tensor_tensor(
+            words_view(grouped["x1", 0][:]), planes_view(picked[:, :, :HALF]), per_feature(fb_t), ALU.mult
+        )
+        nc.vector.tensor_tensor(
+            words_view(grouped["x2", 0][:]), planes_view(squares[:, :, :HALF]), per_feature(fa_t), ALU.mult
+        )
+        for name in ("niv", "miv"):
+            for h in range(2):
+                nc.scalar.copy(words_view(grouped[name, h][:]), planes_view(raw[name, h][:]))
+        quant["x1", 0] = quantize("x10", grouped["x1", 0])
+        quant["x2", 0] = quantize("x20", grouped["x2", 0])
+        nc.vector.tensor_copy(words_view(grouped["x1", 1][:]), planes_view(x1_planes[:]))
+        nc.vector.tensor_tensor(
+            words_view(grouped["x2", 1][:]), planes_view(squares[:, :, HALF:]), per_feature(fa_t), ALU.mult
+        )
+        quant["x1", 1] = quantize("x11", grouped["x1", 1])
+        quant["x2", 1] = quantize("x21", grouped["x2", 1])
+        for name in ("niv", "miv"):
+            for h in range(2):
+                quant[name, h] = quantize("%s%d" % (name, h), grouped[name, h])
+
+        tiles = I // P
+        banks = [psum.tile([P, M], F32, name="bank%d" % r) for r in range(tiles)]
+        for h in range(2):
+            for r in range(tiles):
+                cols = slice((r % 2) * P, (r % 2 + 1) * P)
+                for k, (xn, wn) in enumerate((("x2", "niv"), ("x1", "miv"))):
+                    nc.tensor.matmul_mx(
+                        out=banks[r][:, h * HALF : (h + 1) * HALF],
+                        lhsT=quant[xn, r // 2][0][:, cols].bitcast(FP8X4),
+                        lhsT_scale=quant[xn, r // 2][1][:, cols],
+                        rhs=quant[wn, h][0][:].bitcast(FP8X4),
+                        rhs_scale=quant[wn, h][1][:],
+                        start=(k == 0),
+                        stop=(k == 1),
+                    )
+
+        con_flat = con_rows[:].rearrange("p n t -> p (n t)")
+        for r in range(tiles):
+            logits = keep.tile([P, M], F32, name="logits%d" % r)
+            neg_max = keep.tile([P, 1], F32, name="neg_max%d" % r)
+            probs = keep.tile([P, M], F32, name="probs%d" % r)
+            total = keep.tile([P, 1], F32, name="total%d" % r)
+            inv = keep.tile([P, 1], F32, name="inv%d" % r)
+            result = keep.tile([P, M], F32, name="result%d" % r)
+            nc.vector.tensor_tensor(logits[:], banks[r][:], con_flat, ALU.add)
+            nc.vector.tensor_reduce(neg_max[:], logits[:], AXIS.X, ALU.max, negate=True)
+            nc.scalar.activation(probs[:], logits[:], ACT.Exp, bias=neg_max[:], accum_out=total[:])
+            nc.vector.reciprocal(inv[:], total[:])
+            engine = nc.vector if r == tiles - 1 else nc.gpsimd
+            engine.tensor_scalar(result[:], probs[:], inv[:], float(M), ALU.mult, ALU.mult)
+            nc.sync.dma_start(out[r * P : (r + 1) * P, :], result[:])

@@ -20,6 +20,8 @@ P = 128
 PACK = 4
 HALF = 256
 RUN = 4
+HALVES = (slice(0, HALF), slice(HALF, 2 * HALF))
+WHOLE = slice(0, 2 * HALF)
 
 
 def planes_view(ap):
@@ -30,6 +32,10 @@ def words_view(ap):
     return ap.rearrange("p (c i) t -> p c t i", i=RUN)
 
 
+def block(b):
+    return slice(b * P, (b + 1) * P)
+
+
 def tile_attend_mixtureresp_kernel(tc, xs, fa, fb, niv, miv, con, offs, out):
     nc = tc.nc
     with ExitStack() as ctx:
@@ -37,109 +43,130 @@ def tile_attend_mixtureresp_kernel(tc, xs, fa, fb, niv, miv, con, offs, out):
         psum = ctx.enter_context(tc.psum_pool(name="psum", bufs=1))
 
         offsets = keep.tile([P, I // 16], U16, name="offsets")
+        con_t = keep.tile([P, PACK], F32, name="con_t")
         nc.sync.dma_start(offsets[:], offs)
+        nc.sync.dma_start(con_t[:], con.rearrange("o (p t) -> p (o t)", t=PACK))
         xs_planes = xs.rearrange("(p t) s -> p t s", t=PACK)
         windows = [keep.tile([P, T], F32, name="window%d" % t) for t in range(PACK)]
         for t in range(PACK):
             nc.sync.dma_start(windows[t][:], xs_planes[:, t, :])
-        fa_t = keep.tile([P, PACK], F32, name="fa_t")
-        fb_t = keep.tile([P, PACK], F32, name="fb_t")
-        con_t = keep.tile([P, PACK], F32, name="con_t")
-        nc.scalar.dma_start(fb_t[:], fb.rearrange("(p t) o -> p (t o)", t=PACK))
-        nc.scalar.dma_start(fa_t[:], fa.rearrange("(p t) o -> p (t o)", t=PACK))
-        nc.scalar.dma_start(con_t[:], con.rearrange("o (p t) -> p (o t)", t=PACK))
         raw = {}
         for name, table in (("niv", niv), ("miv", miv)):
             for h in range(2):
                 raw[name, h] = keep.tile([P, PACK, HALF], F32, name="raw_%s%d" % (name, h))
-                nc.sync.dma_start(
-                    raw[name, h][:],
-                    table.rearrange("(p t) m -> p t m", t=PACK)[:, :, h * HALF : (h + 1) * HALF],
-                )
+                nc.sync.dma_start(raw[name, h][:], table.rearrange("(p t) m -> p t m", t=PACK)[:, :, HALVES[h]])
 
         ident = keep.tile([P, P], F32, name="ident")
         make_identity(nc, ident[:])
+        fa_t = keep.tile([P, PACK], F32, name="fa_t")
+        fb_t = keep.tile([P, PACK], F32, name="fb_t")
+        nc.scalar.dma_start(fb_t[:], fb.rearrange("(p t) o -> p (t o)", t=PACK))
+        nc.scalar.dma_start(fa_t[:], fa.rearrange("(p t) o -> p (t o)", t=PACK))
+
         con_bank = psum.tile([P, PACK, P], F32, name="con_bank")
         for t in range(PACK):
             nc.tensor.transpose(con_bank[:, t, :], con_t[:, t : t + 1].to_broadcast([P, P]), ident[:])
-        con_rows = keep.tile([P, P, PACK], F32, name="con_rows")
-        nc.scalar.activation(con_rows[:], con_bank[:].rearrange("p t n -> p n t"), ACT.Copy)
+        con_rows = keep.tile([P, M], F32, name="con_rows")
+        nc.scalar.activation(
+            con_rows[:].rearrange("p (n t) -> p n t", t=PACK), con_bank[:].rearrange("p t n -> p n t"), ACT.Copy
+        )
 
         picked = keep.tile([P, PACK, I], F32, name="picked")
         squares = keep.tile([P, PACK, I], F32, name="squares")
-        x1_planes = keep.tile([P, PACK, HALF], BF16, name="x1_planes")
+        x1_planes = keep.tile([P, PACK, I], BF16, name="x1_planes")
         for t in range(PACK):
             nc.vector.tensor_copy(picked[:, t, :], windows[t][:].indirect(offsets[:]))
             nc.scalar.activation(squares[:, t, :], picked[:, t, :], ACT.Square)
-            nc.scalar.activation(x1_planes[:, t, :], picked[:, t, HALF:], ACT.Copy, scale=fb_t[:, t : t + 1])
+            nc.scalar.activation(x1_planes[:, t, :], picked[:, t, :], ACT.Copy, scale=fb_t[:, t : t + 1])
 
-        def per_feature(col):
-            return col[:].rearrange("p (a t b) -> p a t b", a=1, b=1).to_broadcast([P, HALF // RUN, PACK, RUN])
+        fa_walk = fa_t[:].rearrange("p (a t b) -> p a t b", a=1, b=1).to_broadcast([P, HALF // RUN, PACK, RUN])
 
-        def quantize(name, grouped):
-            width = grouped.shape[1]
-            codes = keep.tile([P, width], U32, name="codes_" + name, align_bytes=64)
-            scales = keep.tile([P, width], U8, name="scales_" + name, align_bytes=64)
-            nc.vector.quantize_mx(
-                out=codes[:].bitcast(FP8X4), scales=scales[:], in_=grouped[:].rearrange("p w t -> p (w t)")
-            )
-            return codes, scales
-
-        grouped = {}
+        grouped, codes, scales = {}, {}, {}
         for name in ("x1", "x2", "niv", "miv"):
-            for h in range(2):
-                grouped[name, h] = keep.tile([P, HALF, PACK], BF16, name="grouped_%s%d" % (name, h), align_bytes=64)
-        quant = {}
+            codes[name] = keep.tile([P, 2 * HALF], U32, name="codes_" + name, align_bytes=64)
+            scales[name] = keep.tile([P, 2 * HALF], U8, name="scales_" + name, align_bytes=64)
+            grouped[name] = keep.tile([P, 2 * HALF, PACK], BF16, name="grouped_" + name, align_bytes=64)
+        late_x2 = keep.tile([P, HALF, PACK], BF16, name="late_x2", tag="late_x2", align_bytes=64)
 
-        nc.vector.tensor_tensor(
-            words_view(grouped["x1", 0][:]), planes_view(picked[:, :, :HALF]), per_feature(fb_t), ALU.mult
-        )
-        nc.vector.tensor_tensor(
-            words_view(grouped["x2", 0][:]), planes_view(squares[:, :, :HALF]), per_feature(fa_t), ALU.mult
-        )
-        for name in ("niv", "miv"):
-            for h in range(2):
-                nc.scalar.copy(words_view(grouped[name, h][:]), planes_view(raw[name, h][:]))
-        quant["x1", 0] = quantize("x10", grouped["x1", 0])
-        quant["x2", 0] = quantize("x20", grouped["x2", 0])
-        nc.vector.tensor_copy(words_view(grouped["x1", 1][:]), planes_view(x1_planes[:]))
-        nc.vector.tensor_tensor(
-            words_view(grouped["x2", 1][:]), planes_view(squares[:, :, HALF:]), per_feature(fa_t), ALU.mult
-        )
-        quant["x1", 1] = quantize("x11", grouped["x1", 1])
-        quant["x2", 1] = quantize("x21", grouped["x2", 1])
-        for name in ("niv", "miv"):
-            for h in range(2):
-                quant[name, h] = quantize("%s%d" % (name, h), grouped[name, h])
+        def quantize(name, cols, source=None):
+            source = grouped[name][:, cols, :] if source is None else source
+            nc.vector.quantize_mx(
+                out=codes[name][:, cols].bitcast(FP8X4),
+                scales=scales[name][:, cols],
+                in_=source.rearrange("p w t -> p (w t)"),
+            )
 
-        tiles = I // P
-        banks = [psum.tile([P, M], F32, name="bank%d" % r) for r in range(tiles)]
-        for h in range(2):
-            for r in range(tiles):
-                cols = slice((r % 2) * P, (r % 2 + 1) * P)
-                for k, (xn, wn) in enumerate((("x2", "niv"), ("x1", "miv"))):
-                    nc.tensor.matmul_mx(
-                        out=banks[r][:, h * HALF : (h + 1) * HALF],
-                        lhsT=quant[xn, r // 2][0][:, cols].bitcast(FP8X4),
-                        lhsT_scale=quant[xn, r // 2][1][:, cols],
-                        rhs=quant[wn, h][0][:].bitcast(FP8X4),
-                        rhs_scale=quant[wn, h][1][:],
-                        start=(k == 0),
-                        stop=(k == 1),
-                    )
+        def product(acc, stationary, stationary_cols, moving, moving_cols, first):
+            nc.tensor.matmul_mx(
+                out=acc,
+                lhsT=codes[stationary][:, stationary_cols].bitcast(FP8X4),
+                lhsT_scale=scales[stationary][:, stationary_cols],
+                rhs=codes[moving][:, moving_cols].bitcast(FP8X4),
+                rhs_scale=scales[moving][:, moving_cols],
+                start=first,
+                stop=not first,
+            )
 
-        con_flat = con_rows[:].rearrange("p n t -> p (n t)")
-        for r in range(tiles):
-            logits = keep.tile([P, M], F32, name="logits%d" % r)
-            neg_max = keep.tile([P, 1], F32, name="neg_max%d" % r)
+        x2_planes = keep.tile([P, PACK, HALF], BF16, name="x2_planes")
+        nc.vector.tensor_copy(words_view(grouped["niv"][:, HALVES[0], :]), planes_view(raw["niv", 0][:]))
+        for name, h in (("niv", 1), ("miv", 0), ("miv", 1)):
+            nc.scalar.copy(words_view(grouped[name][:, HALVES[h], :]), planes_view(raw[name, h][:]))
+        for t in range(PACK):
+            nc.scalar.activation(x2_planes[:, t, :], squares[:, t, HALVES[1]], ACT.Copy, scale=fa_t[:, t : t + 1])
+        nc.scalar.copy(words_view(late_x2[:]), planes_view(x2_planes[:]))
+
+        banks = [psum.tile([P, M], F32, name="bank%d" % r) for r in range(I // P)]
+        logits = [keep.tile([P, M], F32, name="logits%d" % r) for r in range(I // P)]
+
+        def add_con(r):
+            nc.vector.tensor_tensor(logits[r][:], banks[r][:], con_rows[:], ALU.add)
+
+        def softmax(r):
+            tag = "late_x2" if r == 1 else "neg_max%d" % r
+            neg_max = keep.tile([P, 1], F32, name="neg_max%d" % r, tag=tag, align_bytes=64)
             probs = keep.tile([P, M], F32, name="probs%d" % r)
             total = keep.tile([P, 1], F32, name="total%d" % r)
             inv = keep.tile([P, 1], F32, name="inv%d" % r)
             result = keep.tile([P, M], F32, name="result%d" % r)
-            nc.vector.tensor_tensor(logits[:], banks[r][:], con_flat, ALU.add)
-            nc.vector.tensor_reduce(neg_max[:], logits[:], AXIS.X, ALU.max, negate=True)
-            nc.scalar.activation(probs[:], logits[:], ACT.Exp, bias=neg_max[:], accum_out=total[:])
+            nc.vector.tensor_reduce(neg_max[:], logits[r][:], AXIS.X, ALU.max, negate=True)
+            nc.scalar.activation(probs[:], logits[r][:], ACT.Exp, bias=neg_max[:], accum_out=total[:])
             nc.vector.reciprocal(inv[:], total[:])
-            engine = nc.vector if r == tiles - 1 else nc.gpsimd
-            engine.tensor_scalar(result[:], probs[:], inv[:], float(M), ALU.mult, ALU.mult)
-            nc.sync.dma_start(out[r * P : (r + 1) * P, :], result[:])
+            if r < 2:
+                nc.gpsimd.tensor_scalar(result[:], probs[:], inv[:], float(M), ALU.mult, ALU.mult)
+                nc.sync.dma_start(out[block(r), :], result[:])
+            elif r == 2:
+                nc.vector.tensor_scalar(result[:], probs[:], inv[:], float(M), ALU.mult, ALU.mult)
+                nc.sync.dma_start(out[block(r), :], result[:])
+            else:
+                for cols, queue in zip(HALVES, (nc.sync, nc.scalar)):
+                    nc.vector.tensor_scalar(result[:, cols], probs[:, cols], inv[:], float(M), ALU.mult, ALU.mult)
+                    queue.dma_start(out[block(r), cols], result[:, cols])
+
+        nc.vector.tensor_tensor(
+            words_view(grouped["x2"][:, HALVES[0], :]), planes_view(squares[:, :, HALVES[0]]), fa_walk, ALU.mult
+        )
+        nc.vector.tensor_copy(words_view(grouped["x1"][:, HALVES[0], :]), planes_view(x1_planes[:, :, HALVES[0]]))
+        quantize("x2", HALVES[0])
+        quantize("niv", WHOLE)
+        quantize("x1", HALVES[0])
+        quantize("miv", HALVES[0])
+        quantize("miv", HALVES[1])
+        for r in (0, 1):
+            product(banks[r][:], "x2", block(r), "niv", WHOLE, True)
+        for r in (0, 1):
+            product(banks[r][:], "x1", block(r), "miv", WHOLE, False)
+        nc.vector.tensor_copy(words_view(grouped["x1"][:, HALVES[1], :]), planes_view(x1_planes[:, :, HALVES[1]]))
+        quantize("x1", HALVES[1])
+        quantize("x2", HALVES[1], late_x2[:])
+        for r in (2, 3):
+            product(banks[r][:], "x1", block(r), "miv", WHOLE, True)
+        for r in (2, 3):
+            product(banks[r][:], "x2", block(r), "niv", WHOLE, False)
+        add_con(0)
+        add_con(1)
+        softmax(0)
+        add_con(2)
+        softmax(1)
+        add_con(3)
+        softmax(2)
+        softmax(3)

from contextlib import ExitStack

import concourse.mybir as mybir
from concourse.masks import make_identity

D, T, I, M = 512, 1024, 512, 512
FLOPS = 2 * 2 * D * I * M

F32 = mybir.dt.float32
BF16 = mybir.dt.bfloat16
U32 = mybir.dt.uint32
U16 = mybir.dt.uint16
U8 = mybir.dt.uint8
FP8X4 = mybir.dt.float8_e4m3fn_x4
ALU = mybir.AluOpType
ACT = mybir.ActivationFunctionType
AXIS = mybir.AxisListType

P = 128
PACK = 4
HALF = 256
RUN = 4
HALVES = (slice(0, HALF), slice(HALF, 2 * HALF))
WHOLE = slice(0, 2 * HALF)


def planes_view(ap):
    return ap.rearrange("p t (c i) -> p c t i", i=RUN)


def words_view(ap):
    return ap.rearrange("p (c i) t -> p c t i", i=RUN)


def block(b):
    return slice(b * P, (b + 1) * P)


def tile_attend_mixtureresp_kernel(tc, xs, fa, fb, niv, miv, con, offs, out):
    nc = tc.nc
    with ExitStack() as ctx:
        keep = ctx.enter_context(tc.tile_pool(name="keep", bufs=1))
        psum = ctx.enter_context(tc.psum_pool(name="psum", bufs=1))

        offsets = keep.tile([P, I // 16], U16, name="offsets")
        con_t = keep.tile([P, PACK], F32, name="con_t")
        nc.sync.dma_start(offsets[:], offs)
        nc.sync.dma_start(con_t[:], con.rearrange("o (p t) -> p (o t)", t=PACK))
        xs_planes = xs.rearrange("(p t) s -> p t s", t=PACK)
        windows = [keep.tile([P, T], F32, name="window%d" % t) for t in range(PACK)]
        for t in range(PACK):
            nc.sync.dma_start(windows[t][:], xs_planes[:, t, :])
        raw = {}
        for name, table in (("niv", niv), ("miv", miv)):
            for h in range(2):
                raw[name, h] = keep.tile([P, PACK, HALF], F32, name="raw_%s%d" % (name, h))
                nc.sync.dma_start(raw[name, h][:], table.rearrange("(p t) m -> p t m", t=PACK)[:, :, HALVES[h]])

        ident = keep.tile([P, P], F32, name="ident")
        make_identity(nc, ident[:])
        fa_t = keep.tile([P, PACK], F32, name="fa_t")
        fb_t = keep.tile([P, PACK], F32, name="fb_t")
        nc.scalar.dma_start(fb_t[:], fb.rearrange("(p t) o -> p (t o)", t=PACK))
        nc.scalar.dma_start(fa_t[:], fa.rearrange("(p t) o -> p (t o)", t=PACK))

        con_bank = psum.tile([P, PACK, P], F32, name="con_bank")
        for t in range(PACK):
            nc.tensor.transpose(con_bank[:, t, :], con_t[:, t : t + 1].to_broadcast([P, P]), ident[:])
        con_rows = keep.tile([P, M], F32, name="con_rows")
        nc.scalar.activation(
            con_rows[:].rearrange("p (n t) -> p n t", t=PACK), con_bank[:].rearrange("p t n -> p n t"), ACT.Copy
        )

        picked = keep.tile([P, PACK, I], F32, name="picked")
        squares = keep.tile([P, PACK, I], F32, name="squares")
        x1_planes = keep.tile([P, PACK, I], BF16, name="x1_planes")
        for t in range(PACK):
            nc.vector.tensor_copy(picked[:, t, :], windows[t][:].indirect(offsets[:]))
            nc.scalar.activation(squares[:, t, :], picked[:, t, :], ACT.Square)
            nc.scalar.activation(x1_planes[:, t, :], picked[:, t, :], ACT.Copy, scale=fb_t[:, t : t + 1])

        fa_walk = fa_t[:].rearrange("p (a t b) -> p a t b", a=1, b=1).to_broadcast([P, HALF // RUN, PACK, RUN])

        grouped, codes, scales = {}, {}, {}
        for name in ("x1", "x2", "niv", "miv"):
            codes[name] = keep.tile([P, 2 * HALF], U32, name="codes_" + name, align_bytes=64)
            scales[name] = keep.tile([P, 2 * HALF], U8, name="scales_" + name, align_bytes=64)
            grouped[name] = keep.tile([P, 2 * HALF, PACK], BF16, name="grouped_" + name, align_bytes=64)
        late_x2 = keep.tile([P, HALF, PACK], BF16, name="late_x2", tag="late_x2", align_bytes=64)

        def quantize(name, cols, source=None):
            source = grouped[name][:, cols, :] if source is None else source
            nc.vector.quantize_mx(
                out=codes[name][:, cols].bitcast(FP8X4),
                scales=scales[name][:, cols],
                in_=source.rearrange("p w t -> p (w t)"),
            )

        def product(acc, stationary, stationary_cols, moving, moving_cols, first):
            nc.tensor.matmul_mx(
                out=acc,
                lhsT=codes[stationary][:, stationary_cols].bitcast(FP8X4),
                lhsT_scale=scales[stationary][:, stationary_cols],
                rhs=codes[moving][:, moving_cols].bitcast(FP8X4),
                rhs_scale=scales[moving][:, moving_cols],
                start=first,
                stop=not first,
            )

        x2_planes = keep.tile([P, PACK, HALF], BF16, name="x2_planes")
        nc.vector.tensor_copy(words_view(grouped["niv"][:, HALVES[0], :]), planes_view(raw["niv", 0][:]))
        for name, h in (("niv", 1), ("miv", 0), ("miv", 1)):
            nc.scalar.copy(words_view(grouped[name][:, HALVES[h], :]), planes_view(raw[name, h][:]))
        for t in range(PACK):
            nc.scalar.activation(x2_planes[:, t, :], squares[:, t, HALVES[1]], ACT.Copy, scale=fa_t[:, t : t + 1])
        nc.scalar.copy(words_view(late_x2[:]), planes_view(x2_planes[:]))

        banks = [psum.tile([P, M], F32, name="bank%d" % r) for r in range(I // P)]
        logits = [keep.tile([P, M], F32, name="logits%d" % r) for r in range(I // P)]

        def add_con(r):
            nc.vector.tensor_tensor(logits[r][:], banks[r][:], con_rows[:], ALU.add)

        def softmax(r):
            tag = "late_x2" if r == 1 else "neg_max%d" % r
            neg_max = keep.tile([P, 1], F32, name="neg_max%d" % r, tag=tag, align_bytes=64)
            probs = keep.tile([P, M], F32, name="probs%d" % r)
            total = keep.tile([P, 1], F32, name="total%d" % r)
            inv = keep.tile([P, 1], F32, name="inv%d" % r)
            result = keep.tile([P, M], F32, name="result%d" % r)
            nc.vector.tensor_reduce(neg_max[:], logits[r][:], AXIS.X, ALU.max, negate=True)
            nc.scalar.activation(probs[:], logits[r][:], ACT.Exp, bias=neg_max[:], accum_out=total[:])
            nc.vector.reciprocal(inv[:], total[:])
            if r < 2:
                nc.gpsimd.tensor_scalar(result[:], probs[:], inv[:], float(M), ALU.mult, ALU.mult)
                nc.sync.dma_start(out[block(r), :], result[:])
            elif r == 2:
                nc.vector.tensor_scalar(result[:], probs[:], inv[:], float(M), ALU.mult, ALU.mult)
                nc.sync.dma_start(out[block(r), :], result[:])
            else:
                for cols, queue in zip(HALVES, (nc.sync, nc.scalar)):
                    nc.vector.tensor_scalar(result[:, cols], probs[:, cols], inv[:], float(M), ALU.mult, ALU.mult)
                    queue.dma_start(out[block(r), cols], result[:, cols])

        nc.vector.tensor_tensor(
            words_view(grouped["x2"][:, HALVES[0], :]), planes_view(squares[:, :, HALVES[0]]), fa_walk, ALU.mult
        )
        nc.vector.tensor_copy(words_view(grouped["x1"][:, HALVES[0], :]), planes_view(x1_planes[:, :, HALVES[0]]))
        quantize("x2", HALVES[0])
        quantize("niv", WHOLE)
        quantize("x1", HALVES[0])
        quantize("miv", HALVES[0])
        quantize("miv", HALVES[1])
        for r in (0, 1):
            product(banks[r][:], "x2", block(r), "niv", WHOLE, True)
        for r in (0, 1):
            product(banks[r][:], "x1", block(r), "miv", WHOLE, False)
        nc.vector.tensor_copy(words_view(grouped["x1"][:, HALVES[1], :]), planes_view(x1_planes[:, :, HALVES[1]]))
        quantize("x1", HALVES[1])
        quantize("x2", HALVES[1], late_x2[:])
        for r in (2, 3):
            product(banks[r][:], "x1", block(r), "miv", WHOLE, True)
        for r in (2, 3):
            product(banks[r][:], "x2", block(r), "niv", WHOLE, False)
        add_con(0)
        add_con(1)
        softmax(0)
        add_con(2)
        softmax(1)
        add_con(3)
        softmax(2)
        softmax(3)
